import numpy as np
import ml_dtypes


def mxq(x, axis, fmt="e4m3"):
    dtype, down = {"e4m3": (ml_dtypes.float8_e4m3fn, 7), "e5m2": (ml_dtypes.float8_e5m2, 14)}[fmt]
    v = np.moveaxis(np.asarray(x, np.float32).astype(ml_dtypes.bfloat16).astype(np.float64), axis, -1)
    blocks = v.reshape(v.shape[:-1] + (-1, 32))
    amax = np.abs(blocks).max(-1, keepdims=True)
    byte = np.maximum(np.where(amax > 0, np.frexp(amax)[1] - 1 + 127, 0) - down, 1)
    scale = np.exp2(byte - 127.0)
    codes = (blocks / scale).astype(np.float32).astype(dtype).astype(np.float64)
    return np.moveaxis((codes * scale).reshape(v.shape), -1, axis)


WIDE = False


def mx_kscale(k):
    if not WIDE:
        return np.ones(k)
    levels = np.array([10, -10, 5, -5, 0])
    if k % 512:
        return np.exp2(np.random.permutation(np.resize(levels, k // 32))).repeat(32)
    a = np.empty((k // 512, 16))
    for p in range(k // 512):
        a[p, :8] = np.random.permutation(np.resize(levels, 8))
        for g in range(8):
            far = levels[np.abs(levels - a[p, g]) >= 10]
            a[p, g + 8] = far[np.random.randint(len(far))]
    return np.exp2(a.ravel()).repeat(32)


def f64(x):
    return np.asarray(x).astype(np.float64)


def striped(idx):
    return np.tile(idx.reshape(-1, 16).T, (8, 1)).astype(np.uint16)


def unstriped(offs):
    return offs[:16].T.reshape(-1).astype(np.int64)


def d_relu2(v):
    return 2.0 * np.maximum(v, 0.0)


K, T, E, C, H, N = 128, 2048, 2, 512, 256, 512


def by_expert(wq, xq):
    return np.concatenate([wq[e].T @ xq[:, e * C:(e + 1) * C] for e in range(E)], axis=1)


def setup_inputs():
    n = np.random.standard_normal
    slot_token = np.random.permutation(T)[:E * C]
    s = mx_kscale(N)[:, None]
    z = np.ones(T); z[slot_token] = mx_kscale(E * C)
    return {
        "xT": (n((K, T)) * z[None, :]).astype(np.float32),
        "dyT": (n((N, T)) * s).astype(np.float32),
        "a": n((H, E * C)).astype(np.float32),
        "w2": (n((E, N, H)) / np.sqrt(N) / s[None]).astype(np.float32),
        "gate": np.tile(np.random.uniform(0.2, 1.0, E * C) / z[slot_token], (N, 1)).astype(np.float32),
        "offs": striped(slot_token),
    }


def reference(xT, dyT, a, w2, gate, offs):
    idx = unstriped(offs)
    gq = mxq(f64(gate) * f64(dyT)[:, idx], 0, "e4m3")
    dh = by_expert(mxq(f64(w2), 1, "e4m3"), gq)
    da = mxq(dh * d_relu2(f64(a)), 1, "e4m3")
    xq = mxq(f64(xT)[:, idx], 1, "e4m3")
    return np.stack([(xq[:, e * C:(e + 1) * C] @ da[:, e * C:(e + 1) * C].T) for e in range(E)])

@@ -1,0 +1,222 @@
+from contextlib import ExitStack
+
+import concourse.mybir as mybir
+from concourse.masks import make_identity
+
+K, T, E, C, H, N = 128, 2048, 2, 512, 256, 512
+FLOPS = 2 * E * C * H * (N + K)
+BYTES = 4 * (K * T + N * T + H * E * C + E * N * H + E * C + E * K * H) + 2 * 128 * E * C // 16
+
+F32 = mybir.dt.float32
+BF16 = mybir.dt.bfloat16
+U32 = mybir.dt.uint32
+U16 = mybir.dt.uint16
+U8 = mybir.dt.uint8
+FP8X4 = mybir.dt.float8_e4m3fn_x4
+MULT = mybir.AluOpType.mult
+COPY = mybir.ActivationFunctionType.Copy
+RELU = mybir.ActivationFunctionType.Relu
+
+P = 128
+PACK = 4
+HALVES = H // P
+
+
+def tile_moe_mlp_relu2_kernel(tc, xT, dyT, a, w2, gate, offs, out):
+    nc = tc.nc
+    with ExitStack() as ctx:
+        sb = ctx.enter_context(tc.tile_pool(name="sb", bufs=1))
+        turn = ctx.enter_context(tc.psum_pool(name="turn", bufs=3))
+        sums = ctx.enter_context(tc.psum_pool(name="sums", bufs=3))
+        last = ctx.enter_context(tc.psum_pool(name="last", bufs=2))
+
+        def tile(name, shape, dtype):
+            return sb.tile(shape, dtype, name=name, align_bytes=64)
+
+        offsets = sb.tile([P, E * C // 16], U16, name="offsets")
+        ident = tile("ident", [P, P], F32)
+        x_all = tile("x_all", [P, T], F32)
+        dy_all = [tile("dy_all%d" % j, [P, T], F32) for j in range(PACK)]
+        gates = [tile("gates%d" % e, [P, C], F32) for e in range(E)]
+        w_raw = [tile("w_raw%d" % e, [P, PACK, H], F32) for e in range(E)]
+        a_raw = [[tile("a_raw%d%d" % (e, h), [P, C], F32) for h in range(HALVES)] for e in range(E)]
+        x_slots = [tile("x_slots%d" % e, [P, C], BF16) for e in range(E)]
+        gate_rows = tile("gate_rows", [P, P], F32)
+        gate_cols = tile("gate_cols", [P, E * C // P], F32)
+        g_rows = [tile("g_rows%d" % e, [P, PACK, C], F32) for e in range(E)]
+        slope = [[tile("slope%d%d" % (e, h), [P, P, PACK], F32) for h in range(HALVES)] for e in range(E)]
+        x_bf = tile("x_bf", [P, E * K * PACK], BF16)
+        g_bf = [tile("g_bf%d" % e, [P, C * PACK], BF16) for e in range(E)]
+        w_bf = [tile("w_bf%d" % e, [P, H * PACK], BF16) for e in range(E)]
+        da_bf = [tile("da_bf%d" % e, [P, H * PACK], BF16) for e in range(E)]
+        x_codes = tile("x_codes", [P, E * K], U32)
+        x_scales = tile("x_scales", [P, E * K], U8)
+        g_codes = [tile("g_codes%d" % e, [P, C], U32) for e in range(E)]
+        g_scales = [tile("g_scales%d" % e, [P, C], U8) for e in range(E)]
+        w_codes = [tile("w_codes%d" % e, [P, H], U32) for e in range(E)]
+        w_scales = [tile("w_scales%d" % e, [P, H], U8) for e in range(E)]
+        da_codes = [tile("da_codes%d" % e, [P, H], U32) for e in range(E)]
+        da_scales = [tile("da_scales%d" % e, [P, H], U8) for e in range(E)]
+        result = [tile("result%d" % e, [P, H], F32) for e in range(E)]
+
+        dy_planes = dyT.rearrange("(p j) t -> p j t", j=PACK)
+
+        def spread_gate(first, count):
+            e, c0 = divmod(first, C)
+            bank = turn.tile([P, PACK, P], F32, name="turned")
+            for b in range(count // P):
+                col = first // P + b
+                nc.tensor.transpose(bank[:, b, :], gate_cols[:, col:col + 1].to_broadcast([P, P]), ident[:])
+            nc.scalar.activation(
+                gates[e][:, c0:c0 + count], bank[:].rearrange("p b c -> p (b c)")[:, 0:count], COPY
+            )
+
+        def load_dy(j):
+            nc.sync.dma_start(out=dy_all[j][:], in_=dy_planes[:, j, :])
+
+        def load_w(e):
+            nc.sync.dma_start(out=w_raw[e][:], in_=w2[e].rearrange("(p j) i -> p j i", j=PACK))
+
+        def load_a(e, h):
+            nc.sync.dma_start(out=a_raw[e][h][:], in_=a[h * P:(h + 1) * P, e * C:(e + 1) * C])
+
+        def listed(first, count):
+            return offsets[:, first // 16:(first + count) // 16]
+
+        def turn_slots(src):
+            bank = turn.tile([P, PACK, P], F32, name="turned")
+            for t in range(PACK):
+                nc.tensor.transpose(bank[:, t, :], src[:, t:C:PACK], ident[:])
+            return bank[:].rearrange("p t c -> p c t")
+
+        def gather_x(e):
+            dst = x_slots[e][:].rearrange("k (u p s) -> k p u s", u=2, s=2)
+            nc.vector.tensor_copy(dst, x_all[:].indirect(listed(e * C, C)))
+
+        def round_x(e):
+            pairs = x_slots[e][:].bitcast(F32)
+            bank = turn.tile([P, 2, P], F32, name="turned")
+            for u in range(2):
+                nc.tensor.transpose(bank[:, u, :], pairs[:, u * P:(u + 1) * P], ident[:])
+            dst = x_bf[:, e * K * PACK:(e + 1) * K * PACK].bitcast(F32).rearrange("p (k u) -> p k u", u=2)
+            nc.scalar.copy(dst, bank[:].rearrange("p u k -> p k u"))
+
+        def gather_g(e, j, first, count):
+            nc.vector.tensor_tensor(
+                g_rows[e][:, j, first:first + count],
+                dy_all[j][:].indirect(listed(e * C + first, count)),
+                gates[e][:, first:first + count],
+                MULT,
+            )
+
+        def round_g(e, j0, first, count):
+            ms = slice(first // PACK, (first + count) // PACK)
+            dst = g_bf[e][:].rearrange("p (t m j) -> p m t j", t=PACK, j=PACK)
+            src = g_rows[e][:].rearrange("p j (m t) -> p m t j", t=PACK)
+            nc.scalar.activation(dst[:, ms, :, j0:j0 + 2], src[:, ms, :, j0:j0 + 2], COPY)
+
+        def round_w(e):
+            nc.scalar.activation(
+                w_bf[e][:].rearrange("p (c i j) -> p c j i", i=4, j=PACK),
+                w_raw[e][:].rearrange("p j (c i) -> p c j i", i=4),
+                COPY,
+            )
+
+        def quantize(codes, scales, values):
+            nc.vector.quantize_mx(out=codes.bitcast(FP8X4), scales=scales, in_=values)
+
+        def make_slope(e, h):
+            nc.scalar.activation(slope[e][h][:], turn_slots(a_raw[e][h]), RELU, scale=2.0)
+
+        def make_da(e, h):
+            cols = slice(h * P, (h + 1) * P)
+            bank = sums.tile([P, PACK, P], F32, name="dh")
+            for t in range(PACK):
+                rows = slice(t * P, (t + 1) * P)
+                nc.tensor.matmul_mx(
+                    out=bank[:, t, :],
+                    lhsT=g_codes[e][:, rows].bitcast(FP8X4),
+                    lhsT_scale=g_scales[e][:, rows],
+                    rhs=w_codes[e][:, cols].bitcast(FP8X4),
+                    rhs_scale=w_scales[e][:, cols],
+                    start=True,
+                    stop=True,
+                )
+            dst = da_bf[e][:, h * P * PACK:(h + 1) * P * PACK].rearrange("p (i t) -> p i t", t=PACK)
+            nc.vector.tensor_tensor(dst, bank[:].rearrange("p t i -> p i t"), slope[e][h][:], MULT)
+
+        def finish(e, h):
+            rows = slice(e * K, (e + 1) * K)
+            cols = slice(h * P, (h + 1) * P)
+            quantize(da_codes[e][:, cols], da_scales[e][:, cols], da_bf[e][:, h * P * PACK:(h + 1) * P * PACK])
+            bank = last.tile([P, P], F32, name="dw")
+            nc.tensor.matmul_mx(
+                out=bank[:],
+                lhsT=x_codes[:, rows].bitcast(FP8X4),
+                lhsT_scale=x_scales[:, rows],
+                rhs=da_codes[e][:, cols].bitcast(FP8X4),
+                rhs_scale=da_scales[e][:, cols],
+                start=True,
+                stop=True,
+            )
+            nc.scalar.copy(result[e][:, cols], bank[:])
+            nc.sync.dma_start(out=out[e][:, cols], in_=result[e][:, cols])
+
+        nc.sync.dma_start(offsets[:], offs)
+        nc.sync.dma_start(
+            out=gate_rows[:], in_=gate[0:P * P // (E * C), :].rearrange("r (b c) -> (r b) c", c=P)
+        )
+        for j in range(PACK):
+            load_dy(j)
+        load_w(0)
+        load_a(0, 0)
+        nc.sync.dma_start(out=x_all[:], in_=xT)
+        load_w(1)
+        load_a(0, 1)
+        load_a(1, 0)
+        load_a(1, 1)
+        make_identity(nc, ident[:])
+
+        gate_bank = turn.tile([P, P], F32, name="turned")
+        nc.tensor.transpose(gate_bank[:], gate_rows[:], ident[:])
+        nc.vector.tensor_copy(gate_cols[:], gate_bank[:, 0:E * C // P])
+        spread_gate(0, C // 2)
+        spread_gate(C // 2, C // 2)
+        spread_gate(C, C)
+
+        gather_g(0, 0, 0, C // 2)
+        gather_g(0, 0, C // 2, C // 2)
+        gather_g(1, 0, 0, C)
+        for e in range(E):
+            gather_g(e, 1, 0, C)
+            round_g(e, 0, 0, C)
+        for e in range(E):
+            gather_g(e, 2, 0, C)
+        for e in range(E):
+            for first in range(0, C, C // 2):
+                gather_g(e, 3, first, C // 2)
+                round_g(e, 2, first, C // 2)
+            if e == 0:
+                round_w(0)
+        quantize(g_codes[0][:], g_scales[0][:], g_bf[0][:])
+        quantize(w_codes[0][:], w_scales[0][:], w_bf[0][:])
+        make_slope(0, 0)
+        gather_x(0)
+        quantize(g_codes[1][:], g_scales[1][:], g_bf[1][:])
+        gather_x(1)
+        round_w(1)
+        quantize(w_codes[1][:], w_scales[1][:], w_bf[1][:])
+        round_x(0)
+        make_da(0, 0)
+        make_slope(0, 1)
+        make_da(0, 1)
+        round_x(1)
+        quantize(x_codes[:], x_scales[:], x_bf[:])
+        make_slope(1, 0)
+        make_slope(1, 1)
+        finish(0, 0)
+        make_da(1, 0)
+        finish(0, 1)
+        make_da(1, 1)
+        finish(1, 0)
+        finish(1, 1)

@@ -14,8 +14,9 @@ U16 = mybir.dt.uint16
 U8 = mybir.dt.uint8
 FP8X4 = mybir.dt.float8_e4m3fn_x4
 MULT = mybir.AluOpType.mult
-COPY = mybir.ActivationFunctionType.Copy
+MAX = mybir.AluOpType.max
 RELU = mybir.ActivationFunctionType.Relu
+COPY = mybir.ActivationFunctionType.Copy
 
 P = 128
 PACK = 4
@@ -26,9 +27,8 @@ def tile_moe_mlp_relu2_kernel(tc, xT, dyT, a, w2, gate, offs, out):
     nc = tc.nc
     with ExitStack() as ctx:
         sb = ctx.enter_context(tc.tile_pool(name="sb", bufs=1))
-        turn = ctx.enter_context(tc.psum_pool(name="turn", bufs=3))
-        sums = ctx.enter_context(tc.psum_pool(name="sums", bufs=3))
-        last = ctx.enter_context(tc.psum_pool(name="last", bufs=2))
+        turn = ctx.enter_context(tc.psum_pool(name="turn", bufs=4))
+        sums = ctx.enter_context(tc.psum_pool(name="sums", bufs=1))
 
         def tile(name, shape, dtype):
             return sb.tile(shape, dtype, name=name, align_bytes=64)
@@ -37,14 +37,16 @@ def tile_moe_mlp_relu2_kernel(tc, xT, dyT, a, w2, gate, offs, out):
         ident = tile("ident", [P, P], F32)
         x_all = tile("x_all", [P, T], F32)
         dy_all = [tile("dy_all%d" % j, [P, T], F32) for j in range(PACK)]
-        gates = [tile("gates%d" % e, [P, C], F32) for e in range(E)]
+        gates = tile("gates", [P, E * C], F32)
         w_raw = [tile("w_raw%d" % e, [P, PACK, H], F32) for e in range(E)]
         a_raw = [[tile("a_raw%d%d" % (e, h), [P, C], F32) for h in range(HALVES)] for e in range(E)]
         x_slots = [tile("x_slots%d" % e, [P, C], BF16) for e in range(E)]
+        x_round = tile("x_round", [P, T], BF16)
         gate_rows = tile("gate_rows", [P, P], F32)
         gate_cols = tile("gate_cols", [P, E * C // P], F32)
-        g_rows = [tile("g_rows%d" % e, [P, PACK, C], F32) for e in range(E)]
+        g_rows = tile("g_rows", [P, PACK, E * C], F32)
         slope = [[tile("slope%d%d" % (e, h), [P, P, PACK], F32) for h in range(HALVES)] for e in range(E)]
+        da_rows = [[tile("da_rows%d%d" % (e, h), [P, C], BF16) for h in range(HALVES)] for e in range(E)]
         x_bf = tile("x_bf", [P, E * K * PACK], BF16)
         g_bf = [tile("g_bf%d" % e, [P, C * PACK], BF16) for e in range(E)]
         w_bf = [tile("w_bf%d" % e, [P, H * PACK], BF16) for e in range(E)]
@@ -61,16 +63,6 @@ def tile_moe_mlp_relu2_kernel(tc, xT, dyT, a, w2, gate, offs, out):
 
         dy_planes = dyT.rearrange("(p j) t -> p j t", j=PACK)
 
-        def spread_gate(first, count):
-            e, c0 = divmod(first, C)
-            bank = turn.tile([P, PACK, P], F32, name="turned")
-            for b in range(count // P):
-                col = first // P + b
-                nc.tensor.transpose(bank[:, b, :], gate_cols[:, col:col + 1].to_broadcast([P, P]), ident[:])
-            nc.scalar.activation(
-                gates[e][:, c0:c0 + count], bank[:].rearrange("p b c -> p (b c)")[:, 0:count], COPY
-            )
-
         def load_dy(j):
             nc.sync.dma_start(out=dy_all[j][:], in_=dy_planes[:, j, :])
 
@@ -83,140 +75,235 @@ def tile_moe_mlp_relu2_kernel(tc, xT, dyT, a, w2, gate, offs, out):
         def listed(first, count):
             return offsets[:, first // 16:(first + count) // 16]
 
-        def turn_slots(src):
+        banks = {}
+        slots_stationary = [False,False]
+
+        def copy(dst, src, on_vector):
+            if on_vector:
+                nc.vector.tensor_copy(dst, src)
+            else:
+                nc.scalar.copy(dst, src)
+
+        def convert(dst, src, on_vector, scale=1.0):
+            if on_vector and scale == 1.0:
+                nc.vector.tensor_copy(dst, src)
+            elif on_vector:
+                nc.vector.tensor_scalar(dst, src, scale, None, MULT)
+            else:
+                nc.scalar.activation(dst, src, COPY, scale=scale)
+
+        def turn_gate_rows():
+            banks["gate"] = turn.tile([P, P], F32, name="turned")
+            nc.tensor.transpose(banks["gate"][:], gate_rows[:], ident[:])
+
+        def copy_gate_cols():
+            nc.vector.tensor_copy(gate_cols[:], banks["gate"][:, 0:E * C // P])
+
+        def turn_gate(first, count):
             bank = turn.tile([P, PACK, P], F32, name="turned")
-            for t in range(PACK):
-                nc.tensor.transpose(bank[:, t, :], src[:, t:C:PACK], ident[:])
-            return bank[:].rearrange("p t c -> p c t")
+            banks["gate", first] = bank
+            for b in range(count // P):
+                col = first // P + b
+                nc.tensor.transpose(bank[:, b, :], gate_cols[:, col:col + 1].to_broadcast([P, P]), ident[:])
 
-        def gather_x(e):
-            dst = x_slots[e][:].rearrange("k (u p s) -> k p u s", u=2, s=2)
-            nc.vector.tensor_copy(dst, x_all[:].indirect(listed(e * C, C)))
+        def copy_gate(first, count):
+            nc.scalar.activation(
+                gates[:, first:first + count], banks["gate", first][:].rearrange("p b c -> p (b c)")[:, 0:count], COPY
+            )
 
-        def round_x(e):
+        def round_x(half, on_vector):
+            cols = slice(half * T // 2, (half + 1) * T // 2)
+            convert(x_round[:, cols], x_all[:, cols], on_vector)
+
+        def gather_x(e, first, count):
+            dst = x_slots[e][:].rearrange("k (u p b) -> k p u b", u=2, b=2)[:, first // PACK:(first + count) // PACK]
+            nc.scalar.activation(dst, x_round[:].indirect(listed(e * C + first, count)), COPY)
+
+        def turn_x(e):
             pairs = x_slots[e][:].bitcast(F32)
             bank = turn.tile([P, 2, P], F32, name="turned")
+            banks["x", e] = bank
             for u in range(2):
                 nc.tensor.transpose(bank[:, u, :], pairs[:, u * P:(u + 1) * P], ident[:])
-            dst = x_bf[:, e * K * PACK:(e + 1) * K * PACK].bitcast(F32).rearrange("p (k u) -> p k u", u=2)
-            nc.scalar.copy(dst, bank[:].rearrange("p u k -> p k u"))
 
-        def gather_g(e, j, first, count):
-            nc.vector.tensor_tensor(
-                g_rows[e][:, j, first:first + count],
-                dy_all[j][:].indirect(listed(e * C + first, count)),
-                gates[e][:, first:first + count],
-                MULT,
+        def copy_x(e):
+            dst = x_bf[:, e * K * PACK:(e + 1) * K * PACK].bitcast(F32).rearrange("p (k u) -> p k u", u=2)
+            nc.scalar.copy(dst, banks["x", e][:].rearrange("p u k -> p k u"))
+
+        def quantize(codes, scales, values, first, count):
+            cols = slice(first, first + count)
+            nc.vector.quantize_mx(
+                out=codes[:, cols].bitcast(FP8X4),
+                scales=scales[:, cols],
+                in_=values[:, first * PACK:(first + count) * PACK],
             )
 
-        def round_g(e, j0, first, count):
-            ms = slice(first // PACK, (first + count) // PACK)
-            dst = g_bf[e][:].rearrange("p (t m j) -> p m t j", t=PACK, j=PACK)
-            src = g_rows[e][:].rearrange("p j (m t) -> p m t j", t=PACK)
-            nc.scalar.activation(dst[:, ms, :, j0:j0 + 2], src[:, ms, :, j0:j0 + 2], COPY)
+        def gather_g(j, first, count):
+            slots = slice(first, first + count)
+            nc.vector.tensor_tensor(
+                g_rows[:, j, slots], dy_all[j][:].indirect(listed(first, count)), gates[:, slots], MULT
+            )
 
-        def round_w(e):
-            nc.scalar.activation(
+        def round_g(e, j0, first, count, on_vector):
+            rows = g_rows[:, :, e * C:(e + 1) * C]
+            if slots_stationary[e]:
+                ms = slice(first // PACK, (first + count) // PACK)
+                dst = g_bf[e][:].rearrange("p (t m j) -> p m t j", t=PACK, j=PACK)[:, ms, :, j0:j0 + 2]
+                src = rows.rearrange("p j (m t) -> p m t j", t=PACK)[:, ms, :, j0:j0 + 2]
+            else:
+                slots = slice(first, first + count)
+                dst = g_bf[e][:].rearrange("p (c j) -> p c j", j=PACK)[:, slots, j0:j0 + 2]
+                src = rows.rearrange("p j c -> p c j")[:, slots, j0:j0 + 2]
+            convert(dst, src, on_vector)
+
+        def round_w(e, on_vector):
+            convert(
                 w_bf[e][:].rearrange("p (c i j) -> p c j i", i=4, j=PACK),
                 w_raw[e][:].rearrange("p j (c i) -> p c j i", i=4),
-                COPY,
+                on_vector,
+                1.0 if slots_stationary[e] else 2.0,
             )
 
-        def quantize(codes, scales, values):
-            nc.vector.quantize_mx(out=codes.bitcast(FP8X4), scales=scales, in_=values)
-
-        def make_slope(e, h):
-            nc.scalar.activation(slope[e][h][:], turn_slots(a_raw[e][h]), RELU, scale=2.0)
-
-        def make_da(e, h):
-            cols = slice(h * P, (h + 1) * P)
-            bank = sums.tile([P, PACK, P], F32, name="dh")
+        def turn_a(e, h):
+            bank = turn.tile([P, PACK, P], F32, name="turned")
+            banks["a", e, h] = bank
             for t in range(PACK):
-                rows = slice(t * P, (t + 1) * P)
-                nc.tensor.matmul_mx(
-                    out=bank[:, t, :],
-                    lhsT=g_codes[e][:, rows].bitcast(FP8X4),
-                    lhsT_scale=g_scales[e][:, rows],
-                    rhs=w_codes[e][:, cols].bitcast(FP8X4),
-                    rhs_scale=w_scales[e][:, cols],
-                    start=True,
-                    stop=True,
-                )
-            dst = da_bf[e][:, h * P * PACK:(h + 1) * P * PACK].rearrange("p (i t) -> p i t", t=PACK)
-            nc.vector.tensor_tensor(dst, bank[:].rearrange("p t i -> p i t"), slope[e][h][:], MULT)
+                nc.tensor.transpose(bank[:, t, :], a_raw[e][h][:, t:C:PACK], ident[:])
 
-        def finish(e, h):
-            rows = slice(e * K, (e + 1) * K)
-            cols = slice(h * P, (h + 1) * P)
-            quantize(da_codes[e][:, cols], da_scales[e][:, cols], da_bf[e][:, h * P * PACK:(h + 1) * P * PACK])
-            bank = last.tile([P, P], F32, name="dw")
+        def make_slope(e, h, on_vector):
+            src = banks["a", e, h][:].rearrange("p t c -> p c t")
+            if on_vector:
+                nc.vector.tensor_scalar(slope[e][h][:], src, 0.0, 2.0, MAX, MULT)
+            else:
+                nc.scalar.activation(slope[e][h][:], src, RELU, scale=2.0)
+
+        def mx(dst, left, left_scales, left_cols, right, right_scales, right_cols):
             nc.tensor.matmul_mx(
-                out=bank[:],
-                lhsT=x_codes[:, rows].bitcast(FP8X4),
-                lhsT_scale=x_scales[:, rows],
-                rhs=da_codes[e][:, cols].bitcast(FP8X4),
-                rhs_scale=da_scales[e][:, cols],
+                out=dst,
+                lhsT=left[:, left_cols].bitcast(FP8X4),
+                lhsT_scale=left_scales[:, left_cols],
+                rhs=right[:, right_cols].bitcast(FP8X4),
+                rhs_scale=right_scales[:, right_cols],
                 start=True,
                 stop=True,
             )
-            nc.scalar.copy(result[e][:, cols], bank[:])
+
+        def make_dh(e, h):
+            cols = slice(h * P, (h + 1) * P)
+            bank = sums.tile([P, C], F32, name="dh", tag="sums%d%d" % (e, h))
+            banks["dh", e, h] = bank
+            if slots_stationary[e]:
+                for t in range(PACK):
+                    rows = slice(t * P, (t + 1) * P)
+                    mx(bank[:, rows], g_codes[e], g_scales[e], rows, w_codes[e], w_scales[e], cols)
+            else:
+                mx(bank[:], w_codes[e], w_scales[e], cols, g_codes[e], g_scales[e], slice(0, C))
+
+        def make_da(e, h):
+            bank = banks["dh", e, h]
+            if slots_stationary[e]:
+                dst = da_bf[e][:, h * P * PACK:(h + 1) * P * PACK].rearrange("p (i t) -> p i t", t=PACK)
+                nc.vector.tensor_tensor(dst, bank[:].rearrange("p (t i) -> p i t", t=PACK), slope[e][h][:], MULT)
+            else:
+                nc.vector.scalar_tensor_tensor(da_rows[e][h][:], a_raw[e][h][:], 0.0, bank[:], MAX, MULT)
+
+        def turn_da(e, h):
+            pairs = da_rows[e][h][:].bitcast(F32)
+            bank = turn.tile([P, 2, P], F32, name="turned")
+            banks["da", e, h] = bank
+            for u in range(2):
+                nc.tensor.transpose(bank[:, u, :], pairs[:, u:C // 2:2], ident[:])
+
+        def copy_da(e, h, on_vector):
+            dst = da_bf[e][:, h * P * PACK:(h + 1) * P * PACK].bitcast(F32).rearrange("p (i u) -> p i u", u=2)
+            copy(dst, banks["da", e, h][:].rearrange("p u i -> p i u"), on_vector)
+
+        def make_dw(e, first, count):
+            bank = sums.tile([P, count], F32, name="dw", tag="sums%d%d" % (e, first // P))
+            banks["dw", e, first] = bank
+            mx(bank[:], x_codes, x_scales, slice(e * K, (e + 1) * K), da_codes[e], da_scales[e], slice(first, first + count))
+
+        def store(e, first, count, on_vector):
+            cols = slice(first, first + count)
+            copy(result[e][:, cols], banks["dw", e, first][:], on_vector)
             nc.sync.dma_start(out=out[e][:, cols], in_=result[e][:, cols])
 
+        nc.sync.dma_start(out=gate_rows[:], in_=gate[0:P * P // (E * C), :].rearrange("r (b c) -> (r b) c", c=P))
         nc.sync.dma_start(offsets[:], offs)
-        nc.sync.dma_start(
-            out=gate_rows[:], in_=gate[0:P * P // (E * C), :].rearrange("r (b c) -> (r b) c", c=P)
-        )
-        for j in range(PACK):
-            load_dy(j)
+        load_dy(0)
+        load_dy(1)
+        load_dy(2)
+        load_dy(3)
         load_w(0)
-        load_a(0, 0)
         nc.sync.dma_start(out=x_all[:], in_=xT)
         load_w(1)
-        load_a(0, 1)
         load_a(1, 0)
         load_a(1, 1)
+        load_a(0, 0)
+        load_a(0, 1)
         make_identity(nc, ident[:])
-
-        gate_bank = turn.tile([P, P], F32, name="turned")
-        nc.tensor.transpose(gate_bank[:], gate_rows[:], ident[:])
-        nc.vector.tensor_copy(gate_cols[:], gate_bank[:, 0:E * C // P])
-        spread_gate(0, C // 2)
-        spread_gate(C // 2, C // 2)
-        spread_gate(C, C)
-
-        gather_g(0, 0, 0, C // 2)
-        gather_g(0, 0, C // 2, C // 2)
-        gather_g(1, 0, 0, C)
-        for e in range(E):
-            gather_g(e, 1, 0, C)
-            round_g(e, 0, 0, C)
-        for e in range(E):
-            gather_g(e, 2, 0, C)
-        for e in range(E):
-            for first in range(0, C, C // 2):
-                gather_g(e, 3, first, C // 2)
-                round_g(e, 2, first, C // 2)
-            if e == 0:
-                round_w(0)
-        quantize(g_codes[0][:], g_scales[0][:], g_bf[0][:])
-        quantize(w_codes[0][:], w_scales[0][:], w_bf[0][:])
-        make_slope(0, 0)
-        gather_x(0)
-        quantize(g_codes[1][:], g_scales[1][:], g_bf[1][:])
-        gather_x(1)
-        round_w(1)
-        quantize(w_codes[1][:], w_scales[1][:], w_bf[1][:])
-        round_x(0)
+        turn_gate_rows()
+        copy_gate_cols()
+        turn_gate(0, 256)
+        copy_gate(0, 256)
+        turn_gate(256, 256)
+        copy_gate(256, 256)
+        turn_gate(512, 512)
+        copy_gate(512, 512)
+        gather_g(0, 0, 256)
+        gather_g(0, 256, 256)
+        gather_g(0, 512, 512)
+        gather_g(1, 0, 512)
+        round_g(0, 0, 0, C, False)
+        gather_g(1, 512, 512)
+        round_g(1, 0, 0, C, False)
+        gather_g(2, 0, 1024)
+        round_w(0, False)
+        gather_g(3, 0, 256)
+        round_g(0, 2, 0, 256, False)
+        gather_g(3, 256, 256)
+        gather_g(3, 768, 256)
+        round_g(0, 2, 256, 256, True)
+        gather_g(3, 512, 256)
+        round_g(1, 2, 256, 256, False)
+        quantize(g_codes[0], g_scales[0], g_bf[0], 0, 512)
+        quantize(w_codes[0], w_scales[0], w_bf[0], 0, H)
+        make_dh(0, 0)
+        round_x(0, True)
+        round_g(1, 2, 0, 256, False)
+        round_w(1, False)
+        quantize(g_codes[1], g_scales[1], g_bf[1], 0, 512)
+        round_x(1, True)
+        quantize(w_codes[1], w_scales[1], w_bf[1], 0, H)
         make_da(0, 0)
-        make_slope(0, 1)
+        make_dh(0, 1)
         make_da(0, 1)
-        round_x(1)
-        quantize(x_codes[:], x_scales[:], x_bf[:])
-        make_slope(1, 0)
-        make_slope(1, 1)
-        finish(0, 0)
+        make_dh(1, 0)
+        gather_x(0, 0, 512)
         make_da(1, 0)
-        finish(0, 1)
+        gather_x(1, 0, 512)
+        make_dh(1, 1)
+        turn_x(0)
+        copy_x(0)
         make_da(1, 1)
-        finish(1, 0)
-        finish(1, 1)
+        turn_da(0, 0)
+        copy_da(0, 0, False)
+        quantize(x_codes, x_scales, x_bf, 0, K)
+        turn_da(0, 1)
+        copy_da(0, 1, True)
+        quantize(da_codes[0], da_scales[0], da_bf[0], 0, 256)
+        turn_da(1, 0)
+        copy_da(1, 0, False)
+        quantize(da_codes[1], da_scales[1], da_bf[1], 0, 128)
+        turn_x(1)
+        turn_da(1, 1)
+        copy_x(1)
+        make_dw(0, 0, 256)
+        quantize(x_codes, x_scales, x_bf, 128, K)
+        copy_da(1, 1, False)
+        make_dw(1, 0, 128)
+        store(0, 0, 256, False)
+        quantize(da_codes[1], da_scales[1], da_bf[1], 128, 128)
+        make_dw(1, 128, 128)
+        store(1, 128, 128, True)
+        store(1, 0, 128, False)

@@ -229,29 +229,29 @@ def tile_moe_mlp_relu2_kernel(tc, xT, dyT, a, w2, gate, offs, out):
             nc.sync.dma_start(out=out[e][:, cols], in_=result[e][:, cols])
 
         nc.sync.dma_start(out=gate_rows[:], in_=gate[0:P * P // (E * C), :].rearrange("r (b c) -> (r b) c", c=P))
-        nc.sync.dma_start(offsets[:], offs)
         load_dy(0)
+        nc.sync.dma_start(offsets[:], offs)
         load_dy(1)
         load_dy(2)
         load_dy(3)
         load_w(0)
         nc.sync.dma_start(out=x_all[:], in_=xT)
         load_w(1)
-        load_a(1, 0)
-        load_a(1, 1)
         load_a(0, 0)
         load_a(0, 1)
+        load_a(1, 0)
+        load_a(1, 1)
         make_identity(nc, ident[:])
         turn_gate_rows()
         copy_gate_cols()
-        turn_gate(0, 256)
-        copy_gate(0, 256)
-        turn_gate(256, 256)
-        copy_gate(256, 256)
+        turn_gate(0, 128)
+        copy_gate(0, 128)
+        turn_gate(128, 384)
+        copy_gate(128, 384)
         turn_gate(512, 512)
         copy_gate(512, 512)
-        gather_g(0, 0, 256)
-        gather_g(0, 256, 256)
+        gather_g(0, 0, 128)
+        gather_g(0, 128, 384)
         gather_g(0, 512, 512)
         gather_g(1, 0, 512)
         round_g(0, 0, 0, C, False)

from contextlib import ExitStack

import concourse.mybir as mybir
from concourse.masks import make_identity

K, T, E, C, H, N = 128, 2048, 2, 512, 256, 512
FLOPS = 2 * E * C * H * (N + K)
BYTES = 4 * (K * T + N * T + H * E * C + E * N * H + E * C + E * K * H) + 2 * 128 * E * C // 16

F32 = mybir.dt.float32
BF16 = mybir.dt.bfloat16
U32 = mybir.dt.uint32
U16 = mybir.dt.uint16
U8 = mybir.dt.uint8
FP8X4 = mybir.dt.float8_e4m3fn_x4
MULT = mybir.AluOpType.mult
MAX = mybir.AluOpType.max
RELU = mybir.ActivationFunctionType.Relu
COPY = mybir.ActivationFunctionType.Copy

P = 128
PACK = 4
HALVES = H // P


def tile_moe_mlp_relu2_kernel(tc, xT, dyT, a, w2, gate, offs, out):
    nc = tc.nc
    with ExitStack() as ctx:
        sb = ctx.enter_context(tc.tile_pool(name="sb", bufs=1))
        turn = ctx.enter_context(tc.psum_pool(name="turn", bufs=4))
        sums = ctx.enter_context(tc.psum_pool(name="sums", bufs=1))

        def tile(name, shape, dtype):
            return sb.tile(shape, dtype, name=name, align_bytes=64)

        offsets = sb.tile([P, E * C // 16], U16, name="offsets")
        ident = tile("ident", [P, P], F32)
        x_all = tile("x_all", [P, T], F32)
        dy_all = [tile("dy_all%d" % j, [P, T], F32) for j in range(PACK)]
        gates = tile("gates", [P, E * C], F32)
        w_raw = [tile("w_raw%d" % e, [P, PACK, H], F32) for e in range(E)]
        a_raw = [[tile("a_raw%d%d" % (e, h), [P, C], F32) for h in range(HALVES)] for e in range(E)]
        x_slots = [tile("x_slots%d" % e, [P, C], BF16) for e in range(E)]
        x_round = tile("x_round", [P, T], BF16)
        gate_rows = tile("gate_rows", [P, P], F32)
        gate_cols = tile("gate_cols", [P, E * C // P], F32)
        g_rows = tile("g_rows", [P, PACK, E * C], F32)
        slope = [[tile("slope%d%d" % (e, h), [P, P, PACK], F32) for h in range(HALVES)] for e in range(E)]
        da_rows = [[tile("da_rows%d%d" % (e, h), [P, C], BF16) for h in range(HALVES)] for e in range(E)]
        x_bf = tile("x_bf", [P, E * K * PACK], BF16)
        g_bf = [tile("g_bf%d" % e, [P, C * PACK], BF16) for e in range(E)]
        w_bf = [tile("w_bf%d" % e, [P, H * PACK], BF16) for e in range(E)]
        da_bf = [tile("da_bf%d" % e, [P, H * PACK], BF16) for e in range(E)]
        x_codes = tile("x_codes", [P, E * K], U32)
        x_scales = tile("x_scales", [P, E * K], U8)
        g_codes = [tile("g_codes%d" % e, [P, C], U32) for e in range(E)]
        g_scales = [tile("g_scales%d" % e, [P, C], U8) for e in range(E)]
        w_codes = [tile("w_codes%d" % e, [P, H], U32) for e in range(E)]
        w_scales = [tile("w_scales%d" % e, [P, H], U8) for e in range(E)]
        da_codes = [tile("da_codes%d" % e, [P, H], U32) for e in range(E)]
        da_scales = [tile("da_scales%d" % e, [P, H], U8) for e in range(E)]
        result = [tile("result%d" % e, [P, H], F32) for e in range(E)]

        dy_planes = dyT.rearrange("(p j) t -> p j t", j=PACK)

        def load_dy(j):
            nc.sync.dma_start(out=dy_all[j][:], in_=dy_planes[:, j, :])

        def load_w(e):
            nc.sync.dma_start(out=w_raw[e][:], in_=w2[e].rearrange("(p j) i -> p j i", j=PACK))

        def load_a(e, h):
            nc.sync.dma_start(out=a_raw[e][h][:], in_=a[h * P:(h + 1) * P, e * C:(e + 1) * C])

        def listed(first, count):
            return offsets[:, first // 16:(first + count) // 16]

        banks = {}
        slots_stationary = [False,False]

        def copy(dst, src, on_vector):
            if on_vector:
                nc.vector.tensor_copy(dst, src)
            else:
                nc.scalar.copy(dst, src)

        def convert(dst, src, on_vector, scale=1.0):
            if on_vector and scale == 1.0:
                nc.vector.tensor_copy(dst, src)
            elif on_vector:
                nc.vector.tensor_scalar(dst, src, scale, None, MULT)
            else:
                nc.scalar.activation(dst, src, COPY, scale=scale)

        def turn_gate_rows():
            banks["gate"] = turn.tile([P, P], F32, name="turned")
            nc.tensor.transpose(banks["gate"][:], gate_rows[:], ident[:])

        def copy_gate_cols():
            nc.vector.tensor_copy(gate_cols[:], banks["gate"][:, 0:E * C // P])

        def turn_gate(first, count):
            bank = turn.tile([P, PACK, P], F32, name="turned")
            banks["gate", first] = bank
            for b in range(count // P):
                col = first // P + b
                nc.tensor.transpose(bank[:, b, :], gate_cols[:, col:col + 1].to_broadcast([P, P]), ident[:])

        def copy_gate(first, count):
            nc.scalar.activation(
                gates[:, first:first + count], banks["gate", first][:].rearrange("p b c -> p (b c)")[:, 0:count], COPY
            )

        def round_x(half, on_vector):
            cols = slice(half * T // 2, (half + 1) * T // 2)
            convert(x_round[:, cols], x_all[:, cols], on_vector)

        def gather_x(e, first, count):
            dst = x_slots[e][:].rearrange("k (u p b) -> k p u b", u=2, b=2)[:, first // PACK:(first + count) // PACK]
            nc.scalar.activation(dst, x_round[:].indirect(listed(e * C + first, count)), COPY)

        def turn_x(e):
            pairs = x_slots[e][:].bitcast(F32)
            bank = turn.tile([P, 2, P], F32, name="turned")
            banks["x", e] = bank
            for u in range(2):
                nc.tensor.transpose(bank[:, u, :], pairs[:, u * P:(u + 1) * P], ident[:])

        def copy_x(e):
            dst = x_bf[:, e * K * PACK:(e + 1) * K * PACK].bitcast(F32).rearrange("p (k u) -> p k u", u=2)
            nc.scalar.copy(dst, banks["x", e][:].rearrange("p u k -> p k u"))

        def quantize(codes, scales, values, first, count):
            cols = slice(first, first + count)
            nc.vector.quantize_mx(
                out=codes[:, cols].bitcast(FP8X4),
                scales=scales[:, cols],
                in_=values[:, first * PACK:(first + count) * PACK],
            )

        def gather_g(j, first, count):
            slots = slice(first, first + count)
            nc.vector.tensor_tensor(
                g_rows[:, j, slots], dy_all[j][:].indirect(listed(first, count)), gates[:, slots], MULT
            )

        def round_g(e, j0, first, count, on_vector):
            rows = g_rows[:, :, e * C:(e + 1) * C]
            if slots_stationary[e]:
                ms = slice(first // PACK, (first + count) // PACK)
                dst = g_bf[e][:].rearrange("p (t m j) -> p m t j", t=PACK, j=PACK)[:, ms, :, j0:j0 + 2]
                src = rows.rearrange("p j (m t) -> p m t j", t=PACK)[:, ms, :, j0:j0 + 2]
            else:
                slots = slice(first, first + count)
                dst = g_bf[e][:].rearrange("p (c j) -> p c j", j=PACK)[:, slots, j0:j0 + 2]
                src = rows.rearrange("p j c -> p c j")[:, slots, j0:j0 + 2]
            convert(dst, src, on_vector)

        def round_w(e, on_vector):
            convert(
                w_bf[e][:].rearrange("p (c i j) -> p c j i", i=4, j=PACK),
                w_raw[e][:].rearrange("p j (c i) -> p c j i", i=4),
                on_vector,
                1.0 if slots_stationary[e] else 2.0,
            )

        def turn_a(e, h):
            bank = turn.tile([P, PACK, P], F32, name="turned")
            banks["a", e, h] = bank
            for t in range(PACK):
                nc.tensor.transpose(bank[:, t, :], a_raw[e][h][:, t:C:PACK], ident[:])

        def make_slope(e, h, on_vector):
            src = banks["a", e, h][:].rearrange("p t c -> p c t")
            if on_vector:
                nc.vector.tensor_scalar(slope[e][h][:], src, 0.0, 2.0, MAX, MULT)
            else:
                nc.scalar.activation(slope[e][h][:], src, RELU, scale=2.0)

        def mx(dst, left, left_scales, left_cols, right, right_scales, right_cols):
            nc.tensor.matmul_mx(
                out=dst,
                lhsT=left[:, left_cols].bitcast(FP8X4),
                lhsT_scale=left_scales[:, left_cols],
                rhs=right[:, right_cols].bitcast(FP8X4),
                rhs_scale=right_scales[:, right_cols],
                start=True,
                stop=True,
            )

        def make_dh(e, h):
            cols = slice(h * P, (h + 1) * P)
            bank = sums.tile([P, C], F32, name="dh", tag="sums%d%d" % (e, h))
            banks["dh", e, h] = bank
            if slots_stationary[e]:
                for t in range(PACK):
                    rows = slice(t * P, (t + 1) * P)
                    mx(bank[:, rows], g_codes[e], g_scales[e], rows, w_codes[e], w_scales[e], cols)
            else:
                mx(bank[:], w_codes[e], w_scales[e], cols, g_codes[e], g_scales[e], slice(0, C))

        def make_da(e, h):
            bank = banks["dh", e, h]
            if slots_stationary[e]:
                dst = da_bf[e][:, h * P * PACK:(h + 1) * P * PACK].rearrange("p (i t) -> p i t", t=PACK)
                nc.vector.tensor_tensor(dst, bank[:].rearrange("p (t i) -> p i t", t=PACK), slope[e][h][:], MULT)
            else:
                nc.vector.scalar_tensor_tensor(da_rows[e][h][:], a_raw[e][h][:], 0.0, bank[:], MAX, MULT)

        def turn_da(e, h):
            pairs = da_rows[e][h][:].bitcast(F32)
            bank = turn.tile([P, 2, P], F32, name="turned")
            banks["da", e, h] = bank
            for u in range(2):
                nc.tensor.transpose(bank[:, u, :], pairs[:, u:C // 2:2], ident[:])

        def copy_da(e, h, on_vector):
            dst = da_bf[e][:, h * P * PACK:(h + 1) * P * PACK].bitcast(F32).rearrange("p (i u) -> p i u", u=2)
            copy(dst, banks["da", e, h][:].rearrange("p u i -> p i u"), on_vector)

        def make_dw(e, first, count):
            bank = sums.tile([P, count], F32, name="dw", tag="sums%d%d" % (e, first // P))
            banks["dw", e, first] = bank
            mx(bank[:], x_codes, x_scales, slice(e * K, (e + 1) * K), da_codes[e], da_scales[e], slice(first, first + count))

        def store(e, first, count, on_vector):
            cols = slice(first, first + count)
            copy(result[e][:, cols], banks["dw", e, first][:], on_vector)
            nc.sync.dma_start(out=out[e][:, cols], in_=result[e][:, cols])

        nc.sync.dma_start(out=gate_rows[:], in_=gate[0:P * P // (E * C), :].rearrange("r (b c) -> (r b) c", c=P))
        load_dy(0)
        nc.sync.dma_start(offsets[:], offs)
        load_dy(1)
        load_dy(2)
        load_dy(3)
        load_w(0)
        nc.sync.dma_start(out=x_all[:], in_=xT)
        load_w(1)
        load_a(0, 0)
        load_a(0, 1)
        load_a(1, 0)
        load_a(1, 1)
        make_identity(nc, ident[:])
        turn_gate_rows()
        copy_gate_cols()
        turn_gate(0, 128)
        copy_gate(0, 128)
        turn_gate(128, 384)
        copy_gate(128, 384)
        turn_gate(512, 512)
        copy_gate(512, 512)
        gather_g(0, 0, 128)
        gather_g(0, 128, 384)
        gather_g(0, 512, 512)
        gather_g(1, 0, 512)
        round_g(0, 0, 0, C, False)
        gather_g(1, 512, 512)
        round_g(1, 0, 0, C, False)
        gather_g(2, 0, 1024)
        round_w(0, False)
        gather_g(3, 0, 256)
        round_g(0, 2, 0, 256, False)
        gather_g(3, 256, 256)
        gather_g(3, 768, 256)
        round_g(0, 2, 256, 256, True)
        gather_g(3, 512, 256)
        round_g(1, 2, 256, 256, False)
        quantize(g_codes[0], g_scales[0], g_bf[0], 0, 512)
        quantize(w_codes[0], w_scales[0], w_bf[0], 0, H)
        make_dh(0, 0)
        round_x(0, True)
        round_g(1, 2, 0, 256, False)
        round_w(1, False)
        quantize(g_codes[1], g_scales[1], g_bf[1], 0, 512)
        round_x(1, True)
        quantize(w_codes[1], w_scales[1], w_bf[1], 0, H)
        make_da(0, 0)
        make_dh(0, 1)
        make_da(0, 1)
        make_dh(1, 0)
        gather_x(0, 0, 512)
        make_da(1, 0)
        gather_x(1, 0, 512)
        make_dh(1, 1)
        turn_x(0)
        copy_x(0)
        make_da(1, 1)
        turn_da(0, 0)
        copy_da(0, 0, False)
        quantize(x_codes, x_scales, x_bf, 0, K)
        turn_da(0, 1)
        copy_da(0, 1, True)
        quantize(da_codes[0], da_scales[0], da_bf[0], 0, 256)
        turn_da(1, 0)
        copy_da(1, 0, False)
        quantize(da_codes[1], da_scales[1], da_bf[1], 0, 128)
        turn_x(1)
        turn_da(1, 1)
        copy_x(1)
        make_dw(0, 0, 256)
        quantize(x_codes, x_scales, x_bf, 128, K)
        copy_da(1, 1, False)
        make_dw(1, 0, 128)
        store(0, 0, 256, False)
        quantize(da_codes[1], da_scales[1], da_bf[1], 128, 128)
        make_dw(1, 128, 128)
        store(1, 128, 128, True)
        store(1, 0, 128, False)
